import numpy as np
CORES = [36,164,52,180,100,228,116,244]
N = 8
HOST = [c // 128 for c in CORES]
HS = sorted(set(HOST)); H = len(HS)
R, T = 8192, 1024
def entries(a): return a.T.reshape(-1)
def pack(v, P): return np.ascontiguousarray(np.asarray(v, np.int32).reshape(-1, P).T)
def lists(rng, how):
    A = np.array(HOST); L = [rng.permutation(N * R)[:T] for h in HS]
    if how == "away": L = [R * int(rng.choice(np.flatnonzero(A != h))) + rng.permutation(R)[:T] for h in HS]
    if how == "edge": E = R * np.arange(N); E = np.concatenate([E, E + R - 1]); F = np.setdiff1d(np.arange(N * R), E); L = [rng.permutation(np.concatenate([E, rng.permutation(F)[:T - 2 * N]])) for h in HS]
    if how == "home": O = np.repeat(A, R); L = [rng.permutation(np.flatnonzero(O == h))[:T] for h in HS]
    if how == "hotrank": z = R * int(rng.integers(N)); L = [z + rng.permutation(R)[:T] for h in HS]
    if how == "meet": L = [rng.permutation(L[0]) for h in HS]
    return {"idx": np.stack([pack(L[HS.index(HOST[r])], 16) for r in range(N)])}
def setup_inputs(rng):
    return dict({"g": rng.standard_normal((N, 128, T), dtype=np.float32)}, **lists(rng, "uniform"))
def setup_inputs_away(rng):
    d = setup_inputs(rng); d.update(lists(rng, "away"))
    for k in ("g",): d[k] = (d[k].astype(np.float32) * 1024.0).astype(d[k].dtype)
    return d
def setup_inputs_edge(rng):
    d = setup_inputs(rng); d.update(lists(rng, "edge"))
    for k in ("g",): d[k] = (d[k].astype(np.float32) * (1 / 1024.0)).astype(d[k].dtype)
    return d
def setup_inputs_home(rng):
    d = setup_inputs(rng); d.update(lists(rng, "home"))
    return d
def setup_inputs_hotrank(rng):
    d = setup_inputs(rng); d.update(lists(rng, "hotrank"))
    return d
def setup_inputs_meet(rng):
    d = setup_inputs(rng); d.update(lists(rng, "meet"))
    return d
def check_inputs(x):
    bad = []
    if x["idx"].min() < 0 or x["idx"].max() >= N * R: bad.append("idx out of range")
    if any(len(np.unique(a)) != a.size for a in x["idx"]): bad.append("a number stands twice in a list")
    if any(HOST[p] == HOST[s] and not np.array_equal(x["idx"][p], x["idx"][s]) for p in range(N) for s in range(p)): bad.append("two ranks of one host hold different lists")
    return bad
def reference(g, idx):
    S = np.zeros((128, N * R))
    for q in range(N):
        I = entries(idx[q]); S[:, I] += g[q].astype(np.float64)
    return {"y": np.stack([S[:, R * r:R * r + R] for r in range(N)]).astype(np.float32)}

from concourse.bass import DstId, RemoteDMATransfer
from concourse.mybir import dt, AluOpType, AxisListType, ActivationFunctionType

PW = 128
TT = 1024
PART = 8192
WIN = 9344
Q = WIN // 4

SCRATCH = {
    "gs": ("sbuf", [128, TT], "float32"),
    "rs": ("sbuf", [128, 4 * PW], "float32"),
    "t1": ("sbuf", [128, PW], "float32"),
    "t2": ("sbuf", [128, PW], "float32"),
    "sm": ("sbuf", [128, PW], "float32"),
    "tab": ("sbuf", [128, 2 * TT], "float32"),
    "tmp": ("sbuf", [128, TT], "float32"),
    "win": ("sbuf", [128, WIN], "float32"),
    "la": ("sbuf", [128, 64], "int32"),
    "lb": ("sbuf", [128, 64], "int32"),
    "lh": ("sbuf", [128, 64], "int32"),
    "dump": ("sbuf", [128, 64], "int32"),
    "i1": ("sbuf", [128, 64], "int32"),
    "i2": ("sbuf", [128, 64], "int32"),
    "i3": ("sbuf", [128, 64], "int32"),
    "i4": ("sbuf", [128, 64], "int32"),
    "i5": ("sbuf", [128, 64], "int32"),
    "oa": ("sbuf", [128, 64], "uint16"),
    "ob": ("sbuf", [128, 64], "uint16"),
}
SEMAPHORES = (["ga", "gb", "la", "lb", "lh", "iot", "v", "s", "loc", "z", "st"]
              + ["r%d" % i for i in range(4)] + ["p%d" % i for i in range(16)])


def engines(mask):
    return [i for i in range(16) if (mask >> i) & 1]


def split(mask, n):
    e = engines(mask)
    w = len(e) // n
    return [sum(1 << i for i in e[k * w:(k + 1) * w]) for k in range(n)]


def helper_of(c, T, topo):
    for x in range(max(c - 7, 0), c + 8):
        if topo.host(x) != topo.host(c) or topo.chip(x) != topo.chip(c):
            continue
        if topo.die(x) != topo.die(c) and all(topo.may_write(x, d) for d in T.cores):
            return x


def layout(T, topo):
    hosts = sorted(set(topo.host(c) for c in T.cores))
    return [[c for c in T.cores if topo.host(c) == h] for h in hosts]


def dst_id(dst, src, topo):
    rid, pid = topo.addr(dst, src)
    return DstId(rid=rid, pnc=pid)


def common_mask(src, dsts, topo):
    m = 0xFFFF
    for d in dsts:
        m &= topo.mask(src, d)
    return m


def send_sum(g, core, T, topo, groups, hi, k, src):
    peers = [(c, 0) for c in groups[hi] if c != core] + [(c, 1) for c in groups[1 - hi]]
    n = 0
    m = common_mask(core, [c for c, b in peers], topo)
    for half in (0, 1):
        ds = [c for c, b in peers if b == half]
        lo = half * TT + k * PW
        g.remote_dma_fused([RemoteDMATransfer(
            dst_ids=[dst_id(c, core, topo) for c in ds], dma_engine_mask=m,
            remote_sem=T.sem["p%d" % (8 * half + k)], srcs=[src],
            dsts=[T.tab[:, lo:lo + PW] for c in ds])], local_sem=T.sem.loc)
        n += len(engines(m))
    return n


def helper_program(g, core, owner, T, topo):
    groups = layout(T, topo)
    hi = 0 if owner in groups[0] else 1
    a = groups[hi].index(owner)
    partner = groups[1 - hi][a]
    n = 0
    m = topo.mask(core, partner)
    rid, pid = topo.addr(partner, core)
    g.wait_ge(T.sem.lh, len(engines(topo.mask(owner, partner))))
    g.remote_dma(T.lb[:], T.lh[:], T.sem.lb, T.sem.loc, pid, rid, m)
    n += len(engines(m))
    order = [b for b in range(4) if b // 2 != a // 2] + [a ^ 1, a]
    V, v = g.vector, T.sem.v

    def slot(b):
        return T.rs[:, b * PW:(b + 1) * PW]

    cnt = {order[0]: 2, order[1]: 2, order[2]: 4, order[3]: 8}
    V.wait_ge(T.sem["r%d" % order[0]], cnt[order[0]])
    V.wait_ge(T.sem["r%d" % order[1]], cnt[order[1]])
    V.tensor_tensor(T.t1[:], slot(order[0]), slot(order[1]), AluOpType.add).then_inc(v, 1)
    V.wait_ge(T.sem["r%d" % order[2]], cnt[order[2]])
    V.wait_ge(v, 1)
    V.tensor_tensor(T.t2[:], T.t1[:], slot(order[2]), AluOpType.add).then_inc(v, 1)
    V.wait_ge(T.sem["r%d" % order[3]], cnt[order[3]])
    V.wait_ge(v, 2)
    V.tensor_tensor(T.sm[:], T.t2[:], slot(order[3]), AluOpType.add).then_inc(v, 1)
    g.wait_ge(v, 3)
    n += send_sum(g, core, T, topo, groups, hi, 2 * a + 1, T.sm[:])
    g.wait_ge(T.sem.loc, n)


def rank_program(g, core, T, topo):
    rank = T.rank_of(core)
    if rank is None:
        for c in T.cores:
            if helper_of(c, T, topo) == core:
                helper_program(g, core, c, T, topo)
        return
    groups = layout(T, topo)
    hi = 0 if core in groups[0] else 1
    mine = groups[hi]
    a = mine.index(core)
    helper = helper_of(core, T, topo)
    S = T.sem
    V, v = g.vector, T.sem.v
    add = AluOpType.add
    ho = 1 - a // 2
    hs = 1 - ho
    g.sync.dma_start(T.gs[:, 512 * ho:512 * ho + 512], T.g[:, 512 * ho:512 * ho + 512]).then_inc(S.ga, 16)
    g.sync.dma_start(T.gs[:, 512 * hs:512 * hs + 512], T.g[:, 512 * hs:512 * hs + 512]).then_inc(S.gb, 16)
    for q in range(8):
        g.scalar.dma_start(T.la[16 * q:16 * q + 16, :], T.idx[:]).then_inc(S.la, 16)
    g.iota(T.dump[:], [[16, 64]], PART, 1).then_inc(S.iot, 1)
    off = common_mask(core, [c for c in T.cores if c != core], topo)
    n = 0
    g.wait_ge(S.la, 128)
    rid, pid = topo.addr(helper, core)
    g.remote_dma(T.lh[:], T.la[:], S.lh, S.loc, pid, rid, off)
    n += len(engines(off))

    def share(b, w, m):
        d = mine[b] if w == 0 else helper_of(mine[b], T, topo)
        k = 2 * b + w
        return RemoteDMATransfer(dst_ids=[dst_id(d, core, topo)], dma_engine_mask=m, remote_sem=S["r%d" % a],
                                 srcs=[T.gs[:, k * PW:(k + 1) * PW]], dsts=[T.rs[:, a * PW:(a + 1) * PW]])
    m4, m2 = split(off, 4), split(off, 2)
    far = [b for b in range(4) if b // 2 == ho]
    g.wait_ge(S.ga, 16)
    g.remote_dma_fused([share(b, w, m4[2 * i + w]) for i, b in enumerate(far) for w in (0, 1)], local_sem=S.loc)
    g.wait_ge(S.gb, 16)
    g.remote_dma_fused([share(a ^ 1, w, m2[w]) for w in (0, 1)], local_sem=S.loc)
    g.remote_dma_fused([share(a, 1, off)], local_sem=S.loc)
    n += 3 * len(engines(off))
    V.memset(T.win[:, 0:Q], 0.0).then_inc(S.z, 1)
    V.memset(T.win[:, Q:2 * Q], 0.0).then_inc(v, 1)
    g.scalar.wait_ge(S.z, 1)
    for j in (2, 3):
        g.scalar.activation(T.win[:, j * Q:(j + 1) * Q], T.win[:, 0:Q], ActivationFunctionType.Copy).then_inc(S.s, 1)
    nv = [1]

    def op(call):
        call.then_inc(v, 1)
        nv[0] += 1
        V.wait_ge(v, nv[0])

    def offsets(lst, out):
        op(V.tensor_scalar(T.i1[:], lst[:], 13, None, AluOpType.arith_shift_right))
        op(V.tensor_scalar(T.i2[:], T.i1[:], rank, 16384, AluOpType.not_equal, AluOpType.mult))
        op(V.tensor_scalar(T.i3[:], lst[:], PART - 1, None, AluOpType.bitwise_and))
        op(V.tensor_tensor(T.i4[:], T.i3[:], T.i2[:], add))
        op(V.tensor_tensor(T.i5[:], T.i4[:], T.dump[:], AluOpType.min))
        op(V.tensor_copy(out[:], T.i5[:]))
    V.wait_ge(S.la, 128)
    V.wait_ge(S.iot, 1)
    offsets(T.la, T.oa)
    k = 2 * a
    o1, o2 = far
    V.wait_ge(S.gb, 16)
    V.wait_ge(S["r%d" % o1], 2)
    op(V.tensor_tensor(T.t1[:], T.gs[:, k * PW:(k + 1) * PW], T.rs[:, o1 * PW:(o1 + 1) * PW], add))
    V.wait_ge(S["r%d" % o2], 2)
    op(V.tensor_tensor(T.t2[:], T.t1[:], T.rs[:, o2 * PW:(o2 + 1) * PW], add))
    V.wait_ge(S["r%d" % (a ^ 1)], 4)
    own = T.tab[:, k * PW:(k + 1) * PW]
    op(V.tensor_tensor(own, T.t2[:], T.rs[:, (a ^ 1) * PW:((a ^ 1) + 1) * PW], add))
    g.wait_ge(v, nv[0])
    n += send_sum(g, core, T, topo, groups, hi, k, own)
    ne = len(engines(off))
    V.wait_ge(S.lb, ne)
    offsets(T.lb, T.ob)
    V.wait_ge(S.z, 1)
    V.wait_ge(S.s, 2)
    order = [k] + [j for j in range(8) if j != k]
    for j in order:
        if j != k:
            V.wait_ge(S["p%d" % j], ne)
        op(V.tensor_copy(T.win[:, 0:WIN].indirect(T.oa[:, 8 * j:8 * j + 8]), T.tab[:, j * PW:(j + 1) * PW]))
    for j in range(8):
        V.wait_ge(S["p%d" % (8 + j)], ne)
        op(V.tensor_tensor(T.tmp[:, j * PW:(j + 1) * PW], T.win[:, 0:WIN].indirect(T.ob[:, 8 * j:8 * j + 8]),
                           T.tab[:, TT + j * PW:TT + (j + 1) * PW], add))
        op(V.tensor_copy(T.win[:, 0:WIN].indirect(T.ob[:, 8 * j:8 * j + 8]), T.tmp[:, j * PW:(j + 1) * PW]))
    g.sync.wait_ge(v, nv[0])
    g.sync.dma_start(T.y[:], T.win[:, 0:PART]).then_inc(S.st, 16)
    g.sync.wait_ge(S.st, 16)
    g.wait_ge(S.loc, n)
